import numpy as np
import ml_dtypes


def mxq(x, axis, fmt="e4m3"):
    dtype, down = {"e4m3": (ml_dtypes.float8_e4m3fn, 7), "e5m2": (ml_dtypes.float8_e5m2, 14)}[fmt]
    v = np.moveaxis(np.asarray(x, np.float32).astype(ml_dtypes.bfloat16).astype(np.float64), axis, -1)
    blocks = v.reshape(v.shape[:-1] + (-1, 32))
    amax = np.abs(blocks).max(-1, keepdims=True)
    byte = np.maximum(np.where(amax > 0, np.frexp(amax)[1] - 1 + 127, 0) - down, 1)
    scale = np.exp2(byte - 127.0)
    codes = (blocks / scale).astype(np.float32).astype(dtype).astype(np.float64)
    return np.moveaxis((codes * scale).reshape(v.shape), -1, axis)


WIDE = False


def mx_kscale(k):
    if not WIDE:
        return np.ones(k)
    levels = np.array([10, -10, 5, -5, 0])
    if k % 512:
        return np.exp2(np.random.permutation(np.resize(levels, k // 32))).repeat(32)
    a = np.empty((k // 512, 16))
    for p in range(k // 512):
        a[p, :8] = np.random.permutation(np.resize(levels, 8))
        for g in range(8):
            far = levels[np.abs(levels - a[p, g]) >= 10]
            a[p, g + 8] = far[np.random.randint(len(far))]
    return np.exp2(a.ravel()).repeat(32)


def f64(x):
    return np.asarray(x).astype(np.float64)


def striped(idx):
    return np.tile(idx.reshape(-1, 16).T, (8, 1)).astype(np.uint16)


def unstriped(offs):
    return offs[:16].T.reshape(-1).astype(np.int64)


def striped8(idx):
    return np.concatenate([x.reshape(-1, 16).T for x in idx]).astype(np.uint16)


def runs(offs, k):
    lists = np.stack([offs[16 * r : 16 * r + 16].T.reshape(-1) for r in range(8)]).astype(np.int64)
    return lists[np.arange(k) % 512 // 64]


def pack_weight(w):
    k, n = w.shape
    w = f64(np.asarray(w, np.float32).astype(ml_dtypes.bfloat16)).reshape(k // 32, 32, n)
    amax = np.abs(w).max(1)
    byte = np.clip(np.where(amax > 0, np.frexp(amax)[1] - 1 + 127 - 7, 1), 1, 254)
    scaled = (w * np.exp2(127.0 - byte)[:, None, :]).reshape(k, n).astype(np.float32)
    words = np.ascontiguousarray(scaled.reshape(k // 512, 128, 4, n).transpose(0, 1, 3, 2)).astype(ml_dtypes.float8_e4m3fn).view(np.uint8)
    return words, np.ascontiguousarray(byte.astype(np.uint8).reshape(k // 512, 16, n))


def unpack_weight(words, scales):
    g, p, n, _ = words.shape
    vals = np.ascontiguousarray(words).view(ml_dtypes.float8_e4m3fn).astype(np.float64) * np.repeat(np.exp2(scales.astype(np.float64) - 127.0), 8, axis=1)[..., None]
    return vals.transpose(0, 1, 3, 2).reshape(g * 512, n)


K, T, S, H, C = 512, 2048, 256, 512, 512


def setup_inputs():
    n = np.random.standard_normal
    s = mx_kscale(K)[:, None]
    packed_xT = pack_weight(n((K, T)) * s)
    return {
        "x_words": packed_xT[0],
        "x_scales": packed_xT[1],
        "w1": (n((K, H)) / np.sqrt(K) / s).astype(np.float32),
        "w2": (n((K, H)) / np.sqrt(K) / s).astype(np.float32),
        "gs": (np.random.uniform(0.5, 1.5, (K, 1)) / s).astype(np.float32),
        "offs": striped(np.random.permutation(T)[:S]),
        "two": striped(np.random.permutation(T)[:S]),
        "n1": striped(np.random.permutation(S)),
        "n2": striped(np.random.permutation(S)),
        "n3": striped(np.random.permutation(S)),
        "cand": striped(np.random.permutation(T)[:C]),
        "n4": striped8(np.stack([np.random.permutation(S) for _ in range(8)])),
        "n5": striped8(np.stack([np.random.permutation(S) for _ in range(8)])),
    }


def reference(x_words, x_scales, w1, w2, gs, offs, two, n1, n2, n3, cand, n4, n5):
    x_cand = unpack_weight(x_words, x_scales)[:, unstriped(cand)]
    xq = unpack_weight(x_words, x_scales)[:, unstriped(offs)]
    y = mxq(f64(w1), 0, "e4m3").T @ xq
    x_two = unpack_weight(x_words, x_scales)[:, unstriped(two)]
    d = mxq(f64(w2), 0, "e4m3").T @ x_two
    z = f64(gs) * (np.maximum(np.minimum(y - (0.5 * y[:, unstriped(n1)]), d[:, unstriped(n2)]), d[:, unstriped(n3)]))
    s = 0.0625 * ((x_cand.T @ mxq(z, 0, "e4m3")))
    return (s - (s[np.arange(C)[:, None], runs(n4, C)])) / (np.abs(s[np.arange(C)[:, None], runs(n5, C)] - s) + 0.5)

@@ -1,0 +1,224 @@
+from contextlib import ExitStack
+
+import concourse.mybir as mybir
+
+K, T, S, H, C = 512, 2048, 256, 512, 512
+FLOPS = 2 * K * H * S * 2 + 2 * K * C * S
+
+F32 = mybir.dt.float32
+BF16 = mybir.dt.bfloat16
+I32 = mybir.dt.int32
+U32 = mybir.dt.uint32
+U16 = mybir.dt.uint16
+U8 = mybir.dt.uint8
+FP8X4 = mybir.dt.float8_e4m3fn_x4
+ALU = mybir.AluOpType
+ACT = mybir.ActivationFunctionType
+
+P = 128
+PACK = 4
+ONE_LIST_WINDOW = S + 16
+EIGHT_LIST_WINDOW = 2 * S
+HALF = H // 2
+
+
+def tile_picked_twcclampbfrac_none_p_kernel(
+    tc, x_words, x_scales, w1, w2, gs, offs, two, n1, n2, n3, cand, n4, n5, out
+):
+    nc = tc.nc
+    with ExitStack() as ctx:
+        keep = ctx.enter_context(tc.tile_pool(name="keep", bufs=1))
+        stage = ctx.enter_context(tc.tile_pool(name="stage", bufs=1))
+        psum = ctx.enter_context(tc.psum_pool(name="psum", bufs=1))
+
+        def tile(shape, dtype, name):
+            return keep.tile(shape, dtype, name=name, align_bytes=64)
+
+        def staged(shape, dtype, name, offset):
+            return stage.tile(shape, dtype, name=name, align_bytes=64, offset=offset)
+
+        def load_list(dram, name):
+            offsets = tile([P, dram.shape[1]], U16, name)
+            nc.sync.dma_start(offsets[:], dram)
+            return offsets
+
+        def load_weight_half(w, h, name):
+            raw = tile([P, PACK, HALF], F32, name)
+            nc.sync.dma_start(raw[:], w.rearrange("(p j) c -> p j c", j=PACK)[:, :, h * HALF : (h + 1) * HALF])
+            return raw
+
+        x_bytes = tile([P, T], U8, "x_bytes")
+        for q in range(4):
+            nc.sync.dma_start(
+                x_bytes[32 * q : 32 * q + 32, :].bitcast(I32),
+                x_scales[0, 4 * q : 4 * q + 4, :].bitcast(I32).unsqueeze(0).to_broadcast([8, 4, T // 4]),
+            )
+        offs_l = load_list(offs, "offs_l")
+        cand_l = load_list(cand, "cand_l")
+        two_l = load_list(two, "two_l")
+        w1_raw = [load_weight_half(w1, h, "w1_raw%d" % h) for h in range(2)]
+        x_codes = tile([P, T], I32, "x_codes")
+        nc.sync.dma_start(x_codes[:], x_words[0].rearrange("p n t -> p (n t)").bitcast(I32))
+        n1_l = load_list(n1, "n1_l")
+        w2_raw = [load_weight_half(w2, h, "w2_raw%d" % h) for h in range(2)]
+        n2_l = load_list(n2, "n2_l")
+        n3_l = load_list(n3, "n3_l")
+        gain = tile([P, PACK], F32, "gain")
+        nc.sync.dma_start(gain[:], gs.rearrange("(p t) o -> p (t o)", t=PACK))
+        n5_l = load_list(n5, "n5_l")
+        n4_l = load_list(n4, "n4_l")
+
+        def window(width, name):
+            win = tile([P, width], F32, name)
+            nc.gpsimd.memset(win[:, S:], 0.0)
+            return win
+
+        y_win = [window(ONE_LIST_WINDOW, "y_win%d" % t) for t in range(PACK)]
+        d_win = [window(ONE_LIST_WINDOW, "d_win%d" % t) for t in range(PACK)]
+        s_win = [window(EIGHT_LIST_WINDOW, "s_win%d" % t) for t in range(PACK)]
+
+        def pick_scales(offsets, n, name):
+            picked = tile([P, n], U8, name)
+            nc.vector.tensor_copy(picked[:], x_bytes[:].indirect(offsets[:]))
+            return picked
+
+        def pick_codes(offsets, n, name, offset):
+            picked = staged([P, n], U32, name, offset)
+            nc.vector.tensor_copy(picked[:], x_codes[:].bitcast(U32).indirect(offsets[:]))
+            return picked
+
+        def deal(picked, dtype, run, name):
+            dealt = tile([P, C], dtype, name)
+            nc.vector.tensor_copy(
+                dealt[:].rearrange("p (t c i) -> p c t i", t=PACK, i=run),
+                picked[:].rearrange("p (c i t) -> p c t i", t=PACK, i=run),
+            )
+            return dealt
+
+        def group_half(grouped, raw, h, on_scalar):
+            dst = grouped[:].rearrange("p t (m j) -> p m j t", j=PACK)[:, h * 64 : (h + 1) * 64]
+            src = raw[:].rearrange("p j (m t) -> p m j t", t=PACK)
+            if on_scalar:
+                nc.scalar.copy(dst, src)
+            else:
+                nc.vector.tensor_copy(dst, src)
+
+        def quantize_weight(grouped, t, name):
+            codes = tile([P, P], U32, name + "_codes%d" % t)
+            scales = tile([P, P], U8, name + "_scales%d" % t)
+            nc.vector.quantize_mx(out=codes[:].bitcast(FP8X4), scales=scales[:], in_=grouped[:, t, :])
+            return codes, scales
+
+        def multiply(acc, lhs_codes, lhs_scales, rhs_codes, rhs_scales):
+            nc.tensor.matmul_mx(
+                out=acc, lhsT=lhs_codes.bitcast(FP8X4), lhsT_scale=lhs_scales,
+                rhs=rhs_codes.bitcast(FP8X4), rhs_scale=rhs_scales, start=True, stop=True,
+            )
+
+        def look_up(dst, win, offsets):
+            nc.scalar.activation(dst, win[:].indirect(offsets), ACT.Copy)
+
+        q_scales = pick_scales(offs_l, S, "q_scales")
+        c_scales = deal(pick_scales(cand_l, C, "c_scales_raw"), U8, 16, "c_scales")
+        t_scales = pick_scales(two_l, S, "t_scales")
+
+        w1_grouped = staged([P, PACK, P * PACK], BF16, "w1_grouped", 0)
+        group_half(w1_grouped, w1_raw[0], 0, True)
+        group_half(w1_grouped, w1_raw[1], 1, True)
+        w1_mx = [quantize_weight(w1_grouped, t, "w1") for t in range(PACK)]
+        q_codes = pick_codes(offs_l, S, "q_codes", 0)
+        t_codes = pick_codes(two_l, S, "t_codes", 1024)
+
+        y_acc = [psum.tile([P, S], F32, name="y_acc%d" % t) for t in range(PACK)]
+        y_n1 = tile([P, PACK, S], F32, "y_n1")
+        for t in range(PACK):
+            multiply(y_acc[t][:], w1_mx[t][0][:], w1_mx[t][1][:], q_codes[:], q_scales[:])
+            nc.scalar.copy(y_win[t][:, :S], y_acc[t][:])
+            look_up(y_n1[:, t, :], y_win[t], n1_l[:])
+
+        w2_grouped = staged([P, PACK, P * PACK], BF16, "w2_grouped", 2048)
+        diff = tile([P, PACK, S], F32, "diff")
+
+        def difference(t):
+            nc.vector.scalar_tensor_tensor(diff[:, t, :], y_n1[:, t, :], -0.5, y_acc[t][:], ALU.mult, ALU.add)
+
+        group_half(w2_grouped, w2_raw[0], 0, False)
+        difference(0)
+        group_half(w2_grouped, w2_raw[1], 1, False)
+        w2_mx = [quantize_weight(w2_grouped, t, "w2") for t in range(PACK)]
+
+        d_acc = [psum.tile([P, S], F32, name="d_acc%d" % t) for t in range(PACK)]
+        for t in range(PACK):
+            multiply(d_acc[t][:], w2_mx[t][0][:], w2_mx[t][1][:], t_codes[:], t_scales[:])
+        for t in range(2):
+            nc.vector.tensor_copy(d_win[t][:, :S], d_acc[t][:])
+        c_codes = deal(pick_codes(cand_l, C, "c_codes_raw", 4096), U32, 4, "c_codes")
+        for t in range(1, PACK):
+            difference(t)
+
+        d_n2 = tile([P, PACK, S], F32, "d_n2")
+        low = tile([P, PACK, S], F32, "low")
+        for t in range(PACK):
+            if t >= 2:
+                nc.scalar.copy(d_win[t][:, :S], d_acc[t][:])
+            look_up(d_n2[:, t, :], d_win[t], n2_l[:])
+            nc.vector.tensor_tensor(low[:, t, :], diff[:, t, :], d_n2[:, t, :], ALU.min)
+
+        s_acc = [psum.tile([P, S], F32, name="y_acc%d" % t) for t in range(PACK)]
+        half = S // 2
+        for h in range(2):
+            cols = slice(h * half, (h + 1) * half)
+            d_n3 = tile([P, PACK, half], F32, "d_n3_%d" % h)
+            high = tile([P, PACK, half], F32, "high%d" % h)
+            for t in range(PACK):
+                look_up(d_n3[:, t, :], d_win[t], n3_l[:, h * half // 16 : (h + 1) * half // 16])
+                nc.vector.tensor_tensor(high[:, t, :], low[:, t, cols], d_n3[:, t, :], ALU.max)
+            z_grouped = tile([P, half * PACK], BF16, "z_grouped%d" % h)
+            nc.vector.tensor_tensor(
+                z_grouped[:].rearrange("p (c i t) -> p c t i", t=PACK, i=4),
+                high[:].rearrange("p t (c i) -> p c t i", i=4),
+                gain[:].unsqueeze(1).unsqueeze(3).to_broadcast([P, half // 4, PACK, 4]),
+                ALU.mult,
+            )
+            z_codes = tile([P, half], U32, "z_codes%d" % h)
+            z_scales = tile([P, half], U8, "z_scales%d" % h)
+            nc.vector.quantize_mx(out=z_codes[:].bitcast(FP8X4), scales=z_scales[:], in_=z_grouped[:])
+            for t in range(PACK):
+                rows = slice(t * P, (t + 1) * P)
+                multiply(s_acc[t][:, cols], c_codes[:, rows], c_scales[:, rows], z_codes[:], z_scales[:])
+
+        out_rows = out.rearrange("(p t) n -> p t n", t=PACK)
+        nc.scalar.copy(s_win[0][:, :S], s_acc[0][:])
+        for t in range(1, PACK):
+            nc.vector.tensor_copy(s_win[t][:, :S], s_acc[t][:])
+
+        s_n4 = tile([P, PACK, S], F32, "s_n4")
+        s_n5 = tile([P, PACK, S], F32, "s_n5")
+        gap = tile([P, PACK, S], F32, "gap")
+        dist = tile([P, PACK, S], F32, "dist")
+        root = tile([P, PACK, S], F32, "root")
+        recip = tile([P, PACK, S], F32, "recip")
+        num = tile([P, PACK, S], F32, "num")
+        res = tile([P, PACK, S], F32, "res")
+
+        def denominator(t):
+            look_up(s_n5[:, t, :], s_win[t], n5_l[:])
+            nc.vector.tensor_tensor(gap[:, t, :], s_n5[:, t, :], s_acc[t][:], ALU.subtract)
+            nc.vector.scalar_tensor_tensor(dist[:, t, :], gap[:, t, :], -1.0, gap[:, t, :], ALU.mult, ALU.max)
+
+        def inverse(t):
+            nc.scalar.activation(root[:, t, :], dist[:, t, :], ACT.Abs_reciprocal_sqrt, bias=8.0)
+            nc.vector.tensor_tensor(recip[:, t, :], root[:, t, :], root[:, t, :], ALU.mult)
+
+        def quotient(t):
+            look_up(s_n4[:, t, :], s_win[t], n4_l[:])
+            nc.vector.tensor_tensor(num[:, t, :], s_acc[t][:], s_n4[:, t, :], ALU.subtract)
+            nc.vector.tensor_tensor(res[:, t, :], num[:, t, :], recip[:, t, :], ALU.mult)
+            nc.sync.dma_start(out_rows[:, t, :], res[:, t, :])
+
+        denominator(0)
+        for t in range(PACK):
+            if t + 1 < PACK:
+                denominator(t + 1)
+            inverse(t)
+            quotient(t)

@@ -77,6 +77,9 @@ def tile_picked_twcclampbfrac_none_p_kernel(
         d_win = [window(ONE_LIST_WINDOW, "d_win%d" % t) for t in range(PACK)]
         s_win = [window(EIGHT_LIST_WINDOW, "s_win%d" % t) for t in range(PACK)]
 
+        warm = tile([P, 1], F32, "warm")
+        nc.scalar.activation(warm[:], y_win[0][:, S : S + 1], ACT.Abs_reciprocal_sqrt, bias=8.0)
+
         def pick_scales(offsets, n, name):
             picked = tile([P, n], U8, name)
             nc.vector.tensor_copy(picked[:], x_bytes[:].indirect(offsets[:]))
@@ -137,30 +140,27 @@ def tile_picked_twcclampbfrac_none_p_kernel(
             look_up(y_n1[:, t, :], y_win[t], n1_l[:])
 
         w2_grouped = staged([P, PACK, P * PACK], BF16, "w2_grouped", 2048)
-        diff = tile([P, PACK, S], F32, "diff")
+        diff = staged([P, PACK, S], F32, "diff", 5120)
 
         def difference(t):
             nc.vector.scalar_tensor_tensor(diff[:, t, :], y_n1[:, t, :], -0.5, y_acc[t][:], ALU.mult, ALU.add)
 
         group_half(w2_grouped, w2_raw[0], 0, False)
-        difference(0)
         group_half(w2_grouped, w2_raw[1], 1, False)
         w2_mx = [quantize_weight(w2_grouped, t, "w2") for t in range(PACK)]
 
         d_acc = [psum.tile([P, S], F32, name="d_acc%d" % t) for t in range(PACK)]
         for t in range(PACK):
             multiply(d_acc[t][:], w2_mx[t][0][:], w2_mx[t][1][:], t_codes[:], t_scales[:])
-        for t in range(2):
+        for t in range(PACK):
             nc.vector.tensor_copy(d_win[t][:, :S], d_acc[t][:])
-        c_codes = deal(pick_codes(cand_l, C, "c_codes_raw", 4096), U32, 4, "c_codes")
-        for t in range(1, PACK):
+        for t in range(PACK):
             difference(t)
+        c_codes = deal(pick_codes(cand_l, C, "c_codes_raw", 2048), U32, 4, "c_codes")
 
         d_n2 = tile([P, PACK, S], F32, "d_n2")
         low = tile([P, PACK, S], F32, "low")
         for t in range(PACK):
-            if t >= 2:
-                nc.scalar.copy(d_win[t][:, :S], d_acc[t][:])
             look_up(d_n2[:, t, :], d_win[t], n2_l[:])
             nc.vector.tensor_tensor(low[:, t, :], diff[:, t, :], d_n2[:, t, :], ALU.min)
 
@@ -186,39 +186,47 @@ def tile_picked_twcclampbfrac_none_p_kernel(
             for t in range(PACK):
                 rows = slice(t * P, (t + 1) * P)
                 multiply(s_acc[t][:, cols], c_codes[:, rows], c_scales[:, rows], z_codes[:], z_scales[:])
+            for t in range(PACK):
+                if h == 0 or t == 0:
+                    nc.scalar.copy(s_win[t][:, cols], s_acc[t][:, cols])
+                else:
+                    nc.vector.tensor_copy(s_win[t][:, cols], s_acc[t][:, cols])
 
         out_rows = out.rearrange("(p t) n -> p t n", t=PACK)
-        nc.scalar.copy(s_win[0][:, :S], s_acc[0][:])
-        for t in range(1, PACK):
-            nc.vector.tensor_copy(s_win[t][:, :S], s_acc[t][:])
 
-        s_n4 = tile([P, PACK, S], F32, "s_n4")
         s_n5 = tile([P, PACK, S], F32, "s_n5")
         gap = tile([P, PACK, S], F32, "gap")
-        dist = tile([P, PACK, S], F32, "dist")
         root = tile([P, PACK, S], F32, "root")
         recip = tile([P, PACK, S], F32, "recip")
         num = tile([P, PACK, S], F32, "num")
         res = tile([P, PACK, S], F32, "res")
+        dist = [keep.tile([P, S], F32, name="dist%d" % t, tag="slot%d" % (t + 1), align_bytes=64) for t in range(PACK)]
 
-        def denominator(t):
+        for t in range(PACK):
             look_up(s_n5[:, t, :], s_win[t], n5_l[:])
-            nc.vector.tensor_tensor(gap[:, t, :], s_n5[:, t, :], s_acc[t][:], ALU.subtract)
-            nc.vector.scalar_tensor_tensor(dist[:, t, :], gap[:, t, :], -1.0, gap[:, t, :], ALU.mult, ALU.max)
+        for pair in range(0, PACK, 2):
+            for t in (pair, pair + 1):
+                nc.vector.tensor_tensor(gap[:, t, :], s_n5[:, t, :], s_acc[t][:], ALU.subtract)
+            for t in (pair, pair + 1):
+                nc.vector.scalar_tensor_tensor(dist[t][:], gap[:, t, :], -1.0, gap[:, t, :], ALU.mult, ALU.max)
 
-        def inverse(t):
-            nc.scalar.activation(root[:, t, :], dist[:, t, :], ACT.Abs_reciprocal_sqrt, bias=8.0)
-            nc.vector.tensor_tensor(recip[:, t, :], root[:, t, :], root[:, t, :], ALU.mult)
+        s_n4 = []
+        for t in range(PACK):
+            nc.scalar.activation(root[:, t, :], dist[t][:], ACT.Abs_reciprocal_sqrt, bias=8.0)
+            looked = keep.tile([P, S], F32, name="s_n4_%d" % t, tag="slot%d" % t, align_bytes=64)
+            look_up(looked[:], s_win[t], n4_l[:])
+            s_n4.append(looked)
 
         def quotient(t):
-            look_up(s_n4[:, t, :], s_win[t], n4_l[:])
-            nc.vector.tensor_tensor(num[:, t, :], s_acc[t][:], s_n4[:, t, :], ALU.subtract)
             nc.vector.tensor_tensor(res[:, t, :], num[:, t, :], recip[:, t, :], ALU.mult)
             nc.sync.dma_start(out_rows[:, t, :], res[:, t, :])
 
-        denominator(0)
         for t in range(PACK):
             if t + 1 < PACK:
-                denominator(t + 1)
-            inverse(t)
-            quotient(t)
+                nc.vector.tensor_tensor(recip[:, t, :], root[:, t, :], root[:, t, :], ALU.mult)
+            else:
+                nc.scalar.activation(recip[:, t, :], root[:, t, :], ACT.Square)
+            if t > 0:
+                quotient(t - 1)
+            nc.vector.tensor_tensor(num[:, t, :], s_acc[t][:], s_n4[t][:], ALU.subtract)
+        quotient(PACK - 1)

from contextlib import ExitStack

import concourse.mybir as mybir

K, T, S, H, C = 512, 2048, 256, 512, 512
FLOPS = 2 * K * H * S * 2 + 2 * K * C * S

F32 = mybir.dt.float32
BF16 = mybir.dt.bfloat16
I32 = mybir.dt.int32
U32 = mybir.dt.uint32
U16 = mybir.dt.uint16
U8 = mybir.dt.uint8
FP8X4 = mybir.dt.float8_e4m3fn_x4
ALU = mybir.AluOpType
ACT = mybir.ActivationFunctionType

P = 128
PACK = 4
ONE_LIST_WINDOW = S + 16
EIGHT_LIST_WINDOW = 2 * S
HALF = H // 2


def tile_picked_twcclampbfrac_none_p_kernel(
    tc, x_words, x_scales, w1, w2, gs, offs, two, n1, n2, n3, cand, n4, n5, out
):
    nc = tc.nc
    with ExitStack() as ctx:
        keep = ctx.enter_context(tc.tile_pool(name="keep", bufs=1))
        stage = ctx.enter_context(tc.tile_pool(name="stage", bufs=1))
        psum = ctx.enter_context(tc.psum_pool(name="psum", bufs=1))

        def tile(shape, dtype, name):
            return keep.tile(shape, dtype, name=name, align_bytes=64)

        def staged(shape, dtype, name, offset):
            return stage.tile(shape, dtype, name=name, align_bytes=64, offset=offset)

        def load_list(dram, name):
            offsets = tile([P, dram.shape[1]], U16, name)
            nc.sync.dma_start(offsets[:], dram)
            return offsets

        def load_weight_half(w, h, name):
            raw = tile([P, PACK, HALF], F32, name)
            nc.sync.dma_start(raw[:], w.rearrange("(p j) c -> p j c", j=PACK)[:, :, h * HALF : (h + 1) * HALF])
            return raw

        x_bytes = tile([P, T], U8, "x_bytes")
        for q in range(4):
            nc.sync.dma_start(
                x_bytes[32 * q : 32 * q + 32, :].bitcast(I32),
                x_scales[0, 4 * q : 4 * q + 4, :].bitcast(I32).unsqueeze(0).to_broadcast([8, 4, T // 4]),
            )
        offs_l = load_list(offs, "offs_l")
        cand_l = load_list(cand, "cand_l")
        two_l = load_list(two, "two_l")
        w1_raw = [load_weight_half(w1, h, "w1_raw%d" % h) for h in range(2)]
        x_codes = tile([P, T], I32, "x_codes")
        nc.sync.dma_start(x_codes[:], x_words[0].rearrange("p n t -> p (n t)").bitcast(I32))
        n1_l = load_list(n1, "n1_l")
        w2_raw = [load_weight_half(w2, h, "w2_raw%d" % h) for h in range(2)]
        n2_l = load_list(n2, "n2_l")
        n3_l = load_list(n3, "n3_l")
        gain = tile([P, PACK], F32, "gain")
        nc.sync.dma_start(gain[:], gs.rearrange("(p t) o -> p (t o)", t=PACK))
        n5_l = load_list(n5, "n5_l")
        n4_l = load_list(n4, "n4_l")

        def window(width, name):
            win = tile([P, width], F32, name)
            nc.gpsimd.memset(win[:, S:], 0.0)
            return win

        y_win = [window(ONE_LIST_WINDOW, "y_win%d" % t) for t in range(PACK)]
        d_win = [window(ONE_LIST_WINDOW, "d_win%d" % t) for t in range(PACK)]
        s_win = [window(EIGHT_LIST_WINDOW, "s_win%d" % t) for t in range(PACK)]

        warm = tile([P, 1], F32, "warm")
        nc.scalar.activation(warm[:], y_win[0][:, S : S + 1], ACT.Abs_reciprocal_sqrt, bias=8.0)

        def pick_scales(offsets, n, name):
            picked = tile([P, n], U8, name)
            nc.vector.tensor_copy(picked[:], x_bytes[:].indirect(offsets[:]))
            return picked

        def pick_codes(offsets, n, name, offset):
            picked = staged([P, n], U32, name, offset)
            nc.vector.tensor_copy(picked[:], x_codes[:].bitcast(U32).indirect(offsets[:]))
            return picked

        def deal(picked, dtype, run, name):
            dealt = tile([P, C], dtype, name)
            nc.vector.tensor_copy(
                dealt[:].rearrange("p (t c i) -> p c t i", t=PACK, i=run),
                picked[:].rearrange("p (c i t) -> p c t i", t=PACK, i=run),
            )
            return dealt

        def group_half(grouped, raw, h, on_scalar):
            dst = grouped[:].rearrange("p t (m j) -> p m j t", j=PACK)[:, h * 64 : (h + 1) * 64]
            src = raw[:].rearrange("p j (m t) -> p m j t", t=PACK)
            if on_scalar:
                nc.scalar.copy(dst, src)
            else:
                nc.vector.tensor_copy(dst, src)

        def quantize_weight(grouped, t, name):
            codes = tile([P, P], U32, name + "_codes%d" % t)
            scales = tile([P, P], U8, name + "_scales%d" % t)
            nc.vector.quantize_mx(out=codes[:].bitcast(FP8X4), scales=scales[:], in_=grouped[:, t, :])
            return codes, scales

        def multiply(acc, lhs_codes, lhs_scales, rhs_codes, rhs_scales):
            nc.tensor.matmul_mx(
                out=acc, lhsT=lhs_codes.bitcast(FP8X4), lhsT_scale=lhs_scales,
                rhs=rhs_codes.bitcast(FP8X4), rhs_scale=rhs_scales, start=True, stop=True,
            )

        def look_up(dst, win, offsets):
            nc.scalar.activation(dst, win[:].indirect(offsets), ACT.Copy)

        q_scales = pick_scales(offs_l, S, "q_scales")
        c_scales = deal(pick_scales(cand_l, C, "c_scales_raw"), U8, 16, "c_scales")
        t_scales = pick_scales(two_l, S, "t_scales")

        w1_grouped = staged([P, PACK, P * PACK], BF16, "w1_grouped", 0)
        group_half(w1_grouped, w1_raw[0], 0, True)
        group_half(w1_grouped, w1_raw[1], 1, True)
        w1_mx = [quantize_weight(w1_grouped, t, "w1") for t in range(PACK)]
        q_codes = pick_codes(offs_l, S, "q_codes", 0)
        t_codes = pick_codes(two_l, S, "t_codes", 1024)

        y_acc = [psum.tile([P, S], F32, name="y_acc%d" % t) for t in range(PACK)]
        y_n1 = tile([P, PACK, S], F32, "y_n1")
        for t in range(PACK):
            multiply(y_acc[t][:], w1_mx[t][0][:], w1_mx[t][1][:], q_codes[:], q_scales[:])
            nc.scalar.copy(y_win[t][:, :S], y_acc[t][:])
            look_up(y_n1[:, t, :], y_win[t], n1_l[:])

        w2_grouped = staged([P, PACK, P * PACK], BF16, "w2_grouped", 2048)
        diff = staged([P, PACK, S], F32, "diff", 5120)

        def difference(t):
            nc.vector.scalar_tensor_tensor(diff[:, t, :], y_n1[:, t, :], -0.5, y_acc[t][:], ALU.mult, ALU.add)

        group_half(w2_grouped, w2_raw[0], 0, False)
        group_half(w2_grouped, w2_raw[1], 1, False)
        w2_mx = [quantize_weight(w2_grouped, t, "w2") for t in range(PACK)]

        d_acc = [psum.tile([P, S], F32, name="d_acc%d" % t) for t in range(PACK)]
        for t in range(PACK):
            multiply(d_acc[t][:], w2_mx[t][0][:], w2_mx[t][1][:], t_codes[:], t_scales[:])
        for t in range(PACK):
            nc.vector.tensor_copy(d_win[t][:, :S], d_acc[t][:])
        for t in range(PACK):
            difference(t)
        c_codes = deal(pick_codes(cand_l, C, "c_codes_raw", 2048), U32, 4, "c_codes")

        d_n2 = tile([P, PACK, S], F32, "d_n2")
        low = tile([P, PACK, S], F32, "low")
        for t in range(PACK):
            look_up(d_n2[:, t, :], d_win[t], n2_l[:])
            nc.vector.tensor_tensor(low[:, t, :], diff[:, t, :], d_n2[:, t, :], ALU.min)

        s_acc = [psum.tile([P, S], F32, name="y_acc%d" % t) for t in range(PACK)]
        half = S // 2
        for h in range(2):
            cols = slice(h * half, (h + 1) * half)
            d_n3 = tile([P, PACK, half], F32, "d_n3_%d" % h)
            high = tile([P, PACK, half], F32, "high%d" % h)
            for t in range(PACK):
                look_up(d_n3[:, t, :], d_win[t], n3_l[:, h * half // 16 : (h + 1) * half // 16])
                nc.vector.tensor_tensor(high[:, t, :], low[:, t, cols], d_n3[:, t, :], ALU.max)
            z_grouped = tile([P, half * PACK], BF16, "z_grouped%d" % h)
            nc.vector.tensor_tensor(
                z_grouped[:].rearrange("p (c i t) -> p c t i", t=PACK, i=4),
                high[:].rearrange("p t (c i) -> p c t i", i=4),
                gain[:].unsqueeze(1).unsqueeze(3).to_broadcast([P, half // 4, PACK, 4]),
                ALU.mult,
            )
            z_codes = tile([P, half], U32, "z_codes%d" % h)
            z_scales = tile([P, half], U8, "z_scales%d" % h)
            nc.vector.quantize_mx(out=z_codes[:].bitcast(FP8X4), scales=z_scales[:], in_=z_grouped[:])
            for t in range(PACK):
                rows = slice(t * P, (t + 1) * P)
                multiply(s_acc[t][:, cols], c_codes[:, rows], c_scales[:, rows], z_codes[:], z_scales[:])
            for t in range(PACK):
                if h == 0 or t == 0:
                    nc.scalar.copy(s_win[t][:, cols], s_acc[t][:, cols])
                else:
                    nc.vector.tensor_copy(s_win[t][:, cols], s_acc[t][:, cols])

        out_rows = out.rearrange("(p t) n -> p t n", t=PACK)

        s_n5 = tile([P, PACK, S], F32, "s_n5")
        gap = tile([P, PACK, S], F32, "gap")
        root = tile([P, PACK, S], F32, "root")
        recip = tile([P, PACK, S], F32, "recip")
        num = tile([P, PACK, S], F32, "num")
        res = tile([P, PACK, S], F32, "res")
        dist = [keep.tile([P, S], F32, name="dist%d" % t, tag="slot%d" % (t + 1), align_bytes=64) for t in range(PACK)]

        for t in range(PACK):
            look_up(s_n5[:, t, :], s_win[t], n5_l[:])
        for pair in range(0, PACK, 2):
            for t in (pair, pair + 1):
                nc.vector.tensor_tensor(gap[:, t, :], s_n5[:, t, :], s_acc[t][:], ALU.subtract)
            for t in (pair, pair + 1):
                nc.vector.scalar_tensor_tensor(dist[t][:], gap[:, t, :], -1.0, gap[:, t, :], ALU.mult, ALU.max)

        s_n4 = []
        for t in range(PACK):
            nc.scalar.activation(root[:, t, :], dist[t][:], ACT.Abs_reciprocal_sqrt, bias=8.0)
            looked = keep.tile([P, S], F32, name="s_n4_%d" % t, tag="slot%d" % t, align_bytes=64)
            look_up(looked[:], s_win[t], n4_l[:])
            s_n4.append(looked)

        def quotient(t):
            nc.vector.tensor_tensor(res[:, t, :], num[:, t, :], recip[:, t, :], ALU.mult)
            nc.sync.dma_start(out_rows[:, t, :], res[:, t, :])

        for t in range(PACK):
            if t + 1 < PACK:
                nc.vector.tensor_tensor(recip[:, t, :], root[:, t, :], root[:, t, :], ALU.mult)
            else:
                nc.scalar.activation(recip[:, t, :], root[:, t, :], ACT.Square)
            if t > 0:
                quotient(t - 1)
            nc.vector.tensor_tensor(num[:, t, :], s_acc[t][:], s_n4[t][:], ALU.subtract)
        quotient(PACK - 1)
